import numpy as np, ml_dtypes
CORES = [2,42,66,74,82,90,114]
N = 7
import mx_ref
NC, G = 128, 4
C = np.float32(0.047)
BF = ml_dtypes.bfloat16
def cut(t, i, w=512):
    return t[:, w * i:w * i + w]
def tile(rs):
    return np.stack(rs, axis=2).reshape(128, -1).astype(BF)
def layer(w, X):
    out = []
    for i in range(G):
        for t in range(len(X)):
            p = mx_ref.matmul(mx_ref.quantize(cut(w, len(X) * i + t)), X[t])
            z = p if t == 0 else z + p
        out.append(z)
    return out
def masked(A, E):
    return [(e * (a > 0)) * C for a, e in zip(A, E)]
def setup_inputs(rng):
    def f(*shape):
        return mx_ref.flush((rng.standard_normal(shape, dtype=np.float32) * np.exp2(rng.integers(-2, 3, shape[:-1] + (1,)))).astype(BF))
    return {"x": f(N, 128, 512), "e": f(N, 128, 512), "a": f(N, 128, G * 512), "w": f(N, 128, 512), "v": f(N, 128, 4 * NC)}
def setup_inputs_blocks(rng):
    d = setup_inputs(rng)
    for k in ("x", "e", "a", "w", "v"): d[k] = mx_ref.spread(d[k], rng, 2)
    return d
def setup_inputs_wide(rng):
    d = setup_inputs(rng)
    for k in ("x", "e", "a", "w", "v"): d[k] = mx_ref.flush((d[k].astype(np.float32) * np.exp2(rng.integers(-6, 7, (N, 1, 1))).astype(np.float32)).astype(BF))
    return d
def setup_inputs_zeros(rng):
    d = setup_inputs(rng); v = d["x"].reshape(N, 128, -1, 4).copy()
    v[np.broadcast_to((rng.random((N, 1, v.shape[2], 1)) < 0.33), v.shape)] = 0
    d["x"] = v.reshape(d["x"].shape)
    return d
def reference(x, e, a, w, v):
    T = [mx_ref.quantize(tile(masked(layer(a[j], [mx_ref.quantize(x[j])]), layer(a[j], [mx_ref.quantize(e[j])])))) for j in range(N)]
    y = np.zeros((N, 128, N * 128), np.float32); z = np.zeros((N, 128, NC), np.float32)
    for r in range(N):
        qw = mx_ref.quantize(w[r]); qv = mx_ref.quantize(v[r])
        for j in range(N):
            y[r][:, 128 * j:128 * j + 128] = mx_ref.matmul(qw, T[j])
            p = mx_ref.matmul(T[j], qv)
            z[r] = p if j == 0 else z[r] + p
    return {"y": y, "z": z}

@@ -1,0 +1,152 @@
+from concourse.bass import DstId, RemoteDMATransfer
+from concourse.mybir import dt, AluOpType, ActivationFunctionType
+
+N = 7
+C = 0.047
+SCRATCH = {
+    "xe": ("sbuf", [128, 1024], "bfloat16"),
+    "ab": ("sbuf", [128, 2048], "bfloat16"),
+    "wb": ("sbuf", [128, 512], "bfloat16"),
+    "vb": ("sbuf", [128, 512], "bfloat16"),
+    "t": ("sbuf", [128, 512], "bfloat16"),
+    "sg": ("sbuf", [128, 256], "bfloat16"),
+    "m": ("sbuf", [128, 512], "float32"),
+    "yb": ("sbuf", [128, 128 * N], "float32"),
+    "zb": ("sbuf", [128, 128], "float32"),
+    "xq": ("sbuf", [128, 256], "float8_e4m3fn_x4"),
+    "xs": ("sbuf", [128, 256], "uint8"),
+    "aq": ("sbuf", [128, 512], "float8_e4m3fn_x4"),
+    "asc": ("sbuf", [128, 512], "uint8"),
+    "wq": ("sbuf", [128, 128], "float8_e4m3fn_x4"),
+    "ws": ("sbuf", [128, 128], "uint8"),
+    "vq": ("sbuf", [128, 128], "float8_e4m3fn_x4"),
+    "vs": ("sbuf", [128, 128], "uint8"),
+    "tq": ("sbuf", [128, 128 * N], "float8_e4m3fn_x4"),
+    "ts": ("sbuf", [128, 128 * N], "uint8"),
+    "p": ("psum", [128, 512 * 8], "float32"),
+}
+SEMAPHORES = (["ldx", "lde", "ldw", "ldv", "qx", "qe", "qw", "qv", "qt", "sent", "zmm", "zc", "styS", "styA"]
+              + [n + str(i) for n in ("lda", "qa", "um", "mm", "sg", "m", "op") for i in range(4)]
+              + [n + str(j) for n in ("arr", "ymm", "yc") for j in range(N)])
+ON_SCALAR = (0, 1)
+
+
+def rank_program(g, core, T, topo):
+    r = T.rank_of(core)
+    if r is None:
+        return
+    S = T.sem
+    A = ActivationFunctionType
+    col = lambda k, w=128: slice(w * k, w * k + w)
+    bank = lambda k: T.p[:, 512 * k:512 * k + 128]
+    order = [(r - k) % N for k in range(N)]
+    ybank = {j: k + 1 for k, j in enumerate(order)}
+    ZB = 0
+
+    g.sync.dma_start(T.xe[:, 0:512], T.x[:, :]).then_inc(S.ldx, 16)
+    g.scalar.dma_start(T.xe[:, 512:1024], T.e[:, :]).then_inc(S.lde, 16)
+    for i in range(4):
+        q = g.sync if i % 2 == 0 else g.scalar
+        q.dma_start(T.ab[:, col(i, 512)], T.a[:, col(i, 512)]).then_inc(S["lda%d" % i], 16)
+    g.sync.dma_start(T.wb[:, :], T.w[:, :]).then_inc(S.ldw, 16)
+    g.scalar.dma_start(T.vb[:, :], T.v[:, :]).then_inc(S.ldv, 16)
+
+    v = g.vector
+    v.wait_ge(S.ldx, 16)
+    v.quantize_mx(T.xq[:, 0:128], T.xs[:, 0:128], T.xe[:, 0:512]).then_inc(S.qx, 1)
+    v.wait_ge(S.lde, 16)
+    v.quantize_mx(T.xq[:, 128:256], T.xs[:, 128:256], T.xe[:, 512:1024]).then_inc(S.qe, 1)
+    for i in range(4):
+        v.wait_ge(S["lda%d" % i], 16)
+        v.quantize_mx(T.aq[:, col(i)], T.asc[:, col(i)], T.ab[:, col(i, 512)]).then_inc(S["qa%d" % i], 1)
+
+    def factor(i):
+        v.wait_ge(S["um%d" % i], 1)
+        v.tensor_scalar(T.m[:, col(i)], bank(i), 0.0, C, AluOpType.is_gt, AluOpType.mult).then_inc(S["m%d" % i], 1)
+
+    def times(i):
+        v.wait_ge(S["m%d" % i], 1)
+        v.wait_ge(S["mm%d" % i], 1)
+        v.tensor_tensor(T.t[:, i:512:4], bank(4 + i), T.m[:, col(i)], AluOpType.mult).then_inc(S["op%d" % i], 1)
+
+    times(0)
+    factor(2)
+    times(1)
+    factor(3)
+    times(2)
+    times(3)
+    for i in range(4):
+        v.wait_ge(S["op%d" % i], 1)
+    v.quantize_mx(T.tq[:, col(r)], T.ts[:, col(r)], T.t[:, :]).then_inc(S.qt, 1)
+    v.wait_ge(S.ldw, 16)
+    v.quantize_mx(T.wq[:, :], T.ws[:, :], T.wb[:, :]).then_inc(S.qw, 1)
+    v.wait_ge(S.ldv, 16)
+    v.quantize_mx(T.vq[:, :], T.vs[:, :], T.vb[:, :]).then_inc(S.qv, 1)
+
+    for i in ON_SCALAR:
+        g.scalar.wait_ge(S["um%d" % i], 1)
+        g.scalar.activation(T.sg[:, col(i)], bank(i), A.Sign).then_inc(S["sg%d" % i], 1)
+        g.scalar.wait_ge(S["sg%d" % i], 1)
+        g.scalar.activation(T.m[:, col(i)], T.sg[:, col(i)], A.Relu, scale=C).then_inc(S["m%d" % i], 1)
+
+    te = g.tensor
+    te.wait_ge(S.qx, 1)
+    for i in range(4):
+        te.wait_ge(S["qa%d" % i], 1)
+        w, ws = T.aq[:, col(i)], T.asc[:, col(i)]
+        te.matmul_mx(bank(i), w, ws, T.xq[:, 0:128], T.xs[:, 0:128], True, True).then_inc(S["um%d" % i], 1)
+        if i == 0:
+            te.wait_ge(S.qe, 1)
+        te.matmul_mx(bank(4 + i), w, ws, T.xq[:, 128:256], T.xs[:, 128:256], True, True).then_inc(S["mm%d" % i], 1)
+
+    dests = [T.cores[(r + k) % N] for k in range(1, N)]
+    mask = topo.mask(core, dests[0])
+    for d in dests:
+        mask &= topo.mask(core, d)
+    eng = bin(mask).count("1")
+    ids = []
+    for d in dests:
+        rid, pid = topo.addr(d)[:2]
+        ids.append(DstId(rid=rid, pnc=pid))
+    g.wait_ge(S.qt, 1)
+    for ap in (T.ts[:, col(r)], T.tq[:, col(r)].bitcast(dt.uint8)):
+        g.remote_dma_fused([RemoteDMATransfer(dst_ids=ids, dma_engine_mask=mask, remote_sem=S["arr%d" % r],
+                                              src=ap, dsts=[ap for _ in ids])], local_sem=S.sent)
+    g.wait_ge(S.sent, 2 * eng)
+
+    for k, j in enumerate(order):
+        if k == 0:
+            te.wait_ge(S.qt, 1)
+            te.wait_ge(S.qw, 1)
+        else:
+            te.wait_ge(S["arr%d" % j], 2 * eng)
+        q, s = T.tq[:, col(j)], T.ts[:, col(j)]
+        te.matmul_mx(bank(ybank[j]), T.wq[:, :], T.ws[:, :], q, s, True, True).then_inc(S["ymm%d" % j], 1)
+        if k == 0:
+            te.wait_ge(S.qv, 1)
+        mz = te.matmul_mx(bank(ZB), q, s, T.vq[:, :], T.vs[:, :], k == 0, k == N - 1)
+        if k == N - 1:
+            mz.then_inc(S.zmm, 1)
+
+    nS = nA = 0
+    for k, j in enumerate(order):
+        y = T.yb[:, col(j)]
+        if k % 2 == 0:
+            v.wait_ge(S["ymm%d" % j], 1)
+            v.tensor_copy(y, bank(ybank[j])).then_inc(S["yc%d" % j], 1)
+            g.sync.wait_ge(S["yc%d" % j], 1)
+            g.sync.dma_start(T.y[:, col(j)], y).then_inc(S.styS, 16)
+            nS += 16
+        else:
+            g.scalar.wait_ge(S["ymm%d" % j], 1)
+            g.scalar.activation(y, bank(ybank[j]), A.Copy).then_inc(S["yc%d" % j], 1)
+            g.scalar.wait_ge(S["yc%d" % j], 1)
+            g.scalar.dma_start(T.y[:, col(j)], y).then_inc(S.styA, 16)
+            nA += 16
+    g.scalar.wait_ge(S.zmm, 1)
+    g.scalar.activation(T.zb[:, :], bank(ZB), A.Copy).then_inc(S.zc, 1)
+    g.scalar.wait_ge(S.zc, 1)
+    g.scalar.dma_start(T.z[:, :], T.zb[:, :]).then_inc(S.styA, 16)
+    nA += 16
+    g.sync.wait_ge(S.styS, nS)
+    g.scalar.wait_ge(S.styA, nA)

@@ -3,6 +3,7 @@ from concourse.mybir import dt, AluOpType, ActivationFunctionType
 
 N = 7
 C = 0.047
+DIRECT = 4
 SCRATCH = {
     "xe": ("sbuf", [128, 1024], "bfloat16"),
     "ab": ("sbuf", [128, 2048], "bfloat16"),
@@ -25,21 +26,115 @@ SCRATCH = {
     "ts": ("sbuf", [128, 128 * N], "uint8"),
     "p": ("psum", [128, 512 * 8], "float32"),
 }
-SEMAPHORES = (["ldx", "lde", "ldw", "ldv", "qx", "qe", "qw", "qv", "qt", "sent", "zmm", "zc", "styS", "styA"]
+SEMAPHORES = (["ldx", "lde", "ldw", "ldv", "qx", "qe", "qw", "qv", "qt", "sent", "zmm", "zc", "styS", "styA", "hs", "hc"]
               + [n + str(i) for n in ("lda", "qa", "um", "mm", "sg", "m", "op") for i in range(4)]
               + [n + str(j) for n in ("arr", "ymm", "yc") for j in range(N)])
-ON_SCALAR = (0, 1)
+ON_SCALAR = (1, 2)
+PLAN = {}
+
+
+def links(topo, a, b):
+    at, end, d = topo.chip(a), topo.chip(b), topo.die(a)
+    way = []
+    if not topo.same_plane(at, end):
+        way.append(("mate", at, d))
+        at = [c for c in range(topo.CHIPS) if topo.mates(at, c)][0]
+    if at != end:
+        way += [("out", at, d), ("in", end, d)]
+    return frozenset(way)
+
+
+def plan(topo, cores):
+    if "rounds" in PLAN:
+        return PLAN["rounds"]
+    way = {(i, j): links(topo, cores[i], cores[j]) for i in range(N) for j in range(N) if i != j}
+    perms = []
+
+    def extend(perm, used):
+        i = len(perm)
+        if i == N:
+            perms.append(tuple(perm))
+            return
+        for j in range(N):
+            if j != i and j not in perm and not (way[i, j] & used):
+                extend(perm + [j], used | way[i, j])
+
+    extend([], frozenset())
+    perms.sort(key=lambda p: (sum(len(way[i, p[i]]) > 2 for i in range(N)), p))
+
+    def cover(chosen, left):
+        if len(chosen) == N - 1:
+            return chosen
+        for n, p in enumerate(left):
+            rest = [q for q in left[n + 1:] if all(a != b for a, b in zip(p, q))]
+            got = cover(chosen + [p], rest) if len(set(q[0] for q in rest)) == N - 2 - len(chosen) else None
+            if got:
+                return got
+        return None
+
+    PLAN["rounds"] = cover([], perms)[::-1]
+    return PLAN["rounds"]
+
+
+def helper_of(topo, cores, r):
+    for c in range(topo.CHIPS * topo.CORES_PER_CHIP):
+        if (topo.chip(c) == topo.chip(cores[r]) and topo.die(c) != topo.die(cores[r])
+                and all(topo.may_write(c, d) for d in cores)):
+            return c
+
+
+def engines(mask):
+    return bin(mask).count("1")
+
+
+def common(topo, src, dests):
+    mask = topo.mask(src, dests[0])
+    for d in dests:
+        mask &= topo.mask(src, d)
+    return mask
+
+
+def idents(topo, dests):
+    out = []
+    for d in dests:
+        rid, pid = topo.addr(d)[:2]
+        out.append(DstId(rid=rid, pnc=pid))
+    return out
+
+
+def helper_program(g, core, T, topo, r, dests):
+    S = T.sem
+    slot = slice(128 * r, 128 * r + 128)
+    mask = common(topo, core, dests)
+    n_in = engines(spare_engines(topo, T.cores[r], core, T.cores))
+    ids = idents(topo, dests)
+    for sem, ap in ((S.hs, T.ts[:, slot]), (S.hc, T.tq[:, slot].bitcast(dt.uint8))):
+        g.wait_ge(sem, n_in)
+        g.remote_dma_fused([RemoteDMATransfer(dst_ids=ids, dma_engine_mask=mask, remote_sem=S["arr%d" % r],
+                                              src=ap, dsts=[ap for _ in ids])], local_sem=S.sent)
+    g.wait_ge(S.sent, 2 * engines(mask))
+
+
+def spare_engines(topo, src, near, cores):
+    spare = topo.mask(src, near) & ~common(topo, src, [c for c in cores if c != src])
+    bits = [b for b in range(spare.bit_length()) if spare >> b & 1]
+    return sum(1 << b for b in bits[::2])
 
 
 def rank_program(g, core, T, topo):
+    cores = list(T.cores)
+    rounds = plan(topo, cores)
     r = T.rank_of(core)
     if r is None:
+        for j in range(N):
+            if helper_of(topo, cores, j) == core:
+                helper_program(g, core, T, topo, j, [cores[p[j]] for p in rounds[DIRECT:]])
         return
     S = T.sem
     A = ActivationFunctionType
     col = lambda k, w=128: slice(w * k, w * k + w)
     bank = lambda k: T.p[:, 512 * k:512 * k + 128]
-    order = [(r - k) % N for k in range(N)]
+    order = [r] + [p.index(r) for p in rounds]
     ybank = {j: k + 1 for k, j in enumerate(order)}
     ZB = 0
 
@@ -52,11 +147,8 @@ def rank_program(g, core, T, topo):
     g.scalar.dma_start(T.vb[:, :], T.v[:, :]).then_inc(S.ldv, 16)
 
     v = g.vector
-    v.wait_ge(S.ldx, 16)
-    v.quantize_mx(T.xq[:, 0:128], T.xs[:, 0:128], T.xe[:, 0:512]).then_inc(S.qx, 1)
-    v.wait_ge(S.lde, 16)
-    v.quantize_mx(T.xq[:, 128:256], T.xs[:, 128:256], T.xe[:, 512:1024]).then_inc(S.qe, 1)
-    for i in range(4):
+
+    def pack(i):
         v.wait_ge(S["lda%d" % i], 16)
         v.quantize_mx(T.aq[:, col(i)], T.asc[:, col(i)], T.ab[:, col(i, 512)]).then_inc(S["qa%d" % i], 1)
 
@@ -69,8 +161,16 @@ def rank_program(g, core, T, topo):
         v.wait_ge(S["mm%d" % i], 1)
         v.tensor_tensor(T.t[:, i:512:4], bank(4 + i), T.m[:, col(i)], AluOpType.mult).then_inc(S["op%d" % i], 1)
 
+    v.wait_ge(S.ldx, 16)
+    v.quantize_mx(T.xq[:, 0:128], T.xs[:, 0:128], T.xe[:, 0:512]).then_inc(S.qx, 1)
+    v.wait_ge(S.lde, 16)
+    v.quantize_mx(T.xq[:, 128:256], T.xs[:, 128:256], T.xe[:, 512:1024]).then_inc(S.qe, 1)
+    pack(0)
+    pack(1)
+    factor(0)
+    pack(2)
     times(0)
-    factor(2)
+    pack(3)
     times(1)
     factor(3)
     times(2)
@@ -83,11 +183,11 @@ def rank_program(g, core, T, topo):
     v.wait_ge(S.ldv, 16)
     v.quantize_mx(T.vq[:, :], T.vs[:, :], T.vb[:, :]).then_inc(S.qv, 1)
 
-    for i in ON_SCALAR:
+    for n, i in enumerate(ON_SCALAR):
         g.scalar.wait_ge(S["um%d" % i], 1)
-        g.scalar.activation(T.sg[:, col(i)], bank(i), A.Sign).then_inc(S["sg%d" % i], 1)
+        g.scalar.activation(T.sg[:, col(n)], bank(i), A.Sign).then_inc(S["sg%d" % i], 1)
         g.scalar.wait_ge(S["sg%d" % i], 1)
-        g.scalar.activation(T.m[:, col(i)], T.sg[:, col(i)], A.Relu, scale=C).then_inc(S["m%d" % i], 1)
+        g.scalar.activation(T.m[:, col(i)], T.sg[:, col(n)], A.Relu, scale=C).then_inc(S["m%d" % i], 1)
 
     te = g.tensor
     te.wait_ge(S.qx, 1)
@@ -99,20 +199,19 @@ def rank_program(g, core, T, topo):
             te.wait_ge(S.qe, 1)
         te.matmul_mx(bank(4 + i), w, ws, T.xq[:, 128:256], T.xs[:, 128:256], True, True).then_inc(S["mm%d" % i], 1)
 
-    dests = [T.cores[(r + k) % N] for k in range(1, N)]
-    mask = topo.mask(core, dests[0])
-    for d in dests:
-        mask &= topo.mask(core, d)
-    eng = bin(mask).count("1")
-    ids = []
-    for d in dests:
-        rid, pid = topo.addr(d)[:2]
-        ids.append(DstId(rid=rid, pnc=pid))
+    dests = [cores[p[r]] for p in rounds[:DIRECT]]
+    near = helper_of(topo, cores, r)
+    far_mask = common(topo, core, [c for c in cores if c != core])
+    near_mask = spare_engines(topo, core, near, cores)
+    ids, near_id = idents(topo, dests), idents(topo, [near])
+    eng = engines(far_mask)
     g.wait_ge(S.qt, 1)
-    for ap in (T.ts[:, col(r)], T.tq[:, col(r)].bitcast(dt.uint8)):
-        g.remote_dma_fused([RemoteDMATransfer(dst_ids=ids, dma_engine_mask=mask, remote_sem=S["arr%d" % r],
+    for ap, sem in ((T.ts[:, col(r)], S.hs), (T.tq[:, col(r)].bitcast(dt.uint8), S.hc)):
+        g.remote_dma_fused([RemoteDMATransfer(dst_ids=near_id, dma_engine_mask=near_mask, remote_sem=sem,
+                                              src=ap, dsts=[ap]),
+                            RemoteDMATransfer(dst_ids=ids, dma_engine_mask=far_mask, remote_sem=S["arr%d" % r],
                                               src=ap, dsts=[ap for _ in ids])], local_sem=S.sent)
-    g.wait_ge(S.sent, 2 * eng)
+    g.wait_ge(S.sent, 2 * (eng + engines(near_mask)))
 
     for k, j in enumerate(order):
         if k == 0:
@@ -131,7 +230,7 @@ def rank_program(g, core, T, topo):
     nS = nA = 0
     for k, j in enumerate(order):
         y = T.yb[:, col(j)]
-        if k % 2 == 0:
+        if k % 2:
             v.wait_ge(S["ymm%d" % j], 1)
             v.tensor_copy(y, bank(ybank[j])).then_inc(S["yc%d" % j], 1)
             g.sync.wait_ge(S["yc%d" % j], 1)
@@ -143,10 +242,10 @@ def rank_program(g, core, T, topo):
             g.scalar.wait_ge(S["yc%d" % j], 1)
             g.scalar.dma_start(T.y[:, col(j)], y).then_inc(S.styA, 16)
             nA += 16
-    g.scalar.wait_ge(S.zmm, 1)
-    g.scalar.activation(T.zb[:, :], bank(ZB), A.Copy).then_inc(S.zc, 1)
-    g.scalar.wait_ge(S.zc, 1)
-    g.scalar.dma_start(T.z[:, :], T.zb[:, :]).then_inc(S.styA, 16)
-    nA += 16
+    v.wait_ge(S.zmm, 1)
+    v.tensor_copy(T.zb[:, :], bank(ZB)).then_inc(S.zc, 1)
+    g.sync.wait_ge(S.zc, 1)
+    g.sync.dma_start(T.z[:, :], T.zb[:, :]).then_inc(S.styS, 16)
+    nS += 16
     g.sync.wait_ge(S.styS, nS)
     g.scalar.wait_ge(S.styA, nA)

from concourse.bass import DstId, RemoteDMATransfer
from concourse.mybir import dt, AluOpType, ActivationFunctionType

N = 7
C = 0.047
DIRECT = 4
SCRATCH = {
    "xe": ("sbuf", [128, 1024], "bfloat16"),
    "ab": ("sbuf", [128, 2048], "bfloat16"),
    "wb": ("sbuf", [128, 512], "bfloat16"),
    "vb": ("sbuf", [128, 512], "bfloat16"),
    "t": ("sbuf", [128, 512], "bfloat16"),
    "sg": ("sbuf", [128, 256], "bfloat16"),
    "m": ("sbuf", [128, 512], "float32"),
    "yb": ("sbuf", [128, 128 * N], "float32"),
    "zb": ("sbuf", [128, 128], "float32"),
    "xq": ("sbuf", [128, 256], "float8_e4m3fn_x4"),
    "xs": ("sbuf", [128, 256], "uint8"),
    "aq": ("sbuf", [128, 512], "float8_e4m3fn_x4"),
    "asc": ("sbuf", [128, 512], "uint8"),
    "wq": ("sbuf", [128, 128], "float8_e4m3fn_x4"),
    "ws": ("sbuf", [128, 128], "uint8"),
    "vq": ("sbuf", [128, 128], "float8_e4m3fn_x4"),
    "vs": ("sbuf", [128, 128], "uint8"),
    "tq": ("sbuf", [128, 128 * N], "float8_e4m3fn_x4"),
    "ts": ("sbuf", [128, 128 * N], "uint8"),
    "p": ("psum", [128, 512 * 8], "float32"),
}
SEMAPHORES = (["ldx", "lde", "ldw", "ldv", "qx", "qe", "qw", "qv", "qt", "sent", "zmm", "zc", "styS", "styA", "hs", "hc"]
              + [n + str(i) for n in ("lda", "qa", "um", "mm", "sg", "m", "op") for i in range(4)]
              + [n + str(j) for n in ("arr", "ymm", "yc") for j in range(N)])
ON_SCALAR = (1, 2)
PLAN = {}


def links(topo, a, b):
    at, end, d = topo.chip(a), topo.chip(b), topo.die(a)
    way = []
    if not topo.same_plane(at, end):
        way.append(("mate", at, d))
        at = [c for c in range(topo.CHIPS) if topo.mates(at, c)][0]
    if at != end:
        way += [("out", at, d), ("in", end, d)]
    return frozenset(way)


def plan(topo, cores):
    if "rounds" in PLAN:
        return PLAN["rounds"]
    way = {(i, j): links(topo, cores[i], cores[j]) for i in range(N) for j in range(N) if i != j}
    perms = []

    def extend(perm, used):
        i = len(perm)
        if i == N:
            perms.append(tuple(perm))
            return
        for j in range(N):
            if j != i and j not in perm and not (way[i, j] & used):
                extend(perm + [j], used | way[i, j])

    extend([], frozenset())
    perms.sort(key=lambda p: (sum(len(way[i, p[i]]) > 2 for i in range(N)), p))

    def cover(chosen, left):
        if len(chosen) == N - 1:
            return chosen
        for n, p in enumerate(left):
            rest = [q for q in left[n + 1:] if all(a != b for a, b in zip(p, q))]
            got = cover(chosen + [p], rest) if len(set(q[0] for q in rest)) == N - 2 - len(chosen) else None
            if got:
                return got
        return None

    PLAN["rounds"] = cover([], perms)[::-1]
    return PLAN["rounds"]


def helper_of(topo, cores, r):
    for c in range(topo.CHIPS * topo.CORES_PER_CHIP):
        if (topo.chip(c) == topo.chip(cores[r]) and topo.die(c) != topo.die(cores[r])
                and all(topo.may_write(c, d) for d in cores)):
            return c


def engines(mask):
    return bin(mask).count("1")


def common(topo, src, dests):
    mask = topo.mask(src, dests[0])
    for d in dests:
        mask &= topo.mask(src, d)
    return mask


def idents(topo, dests):
    out = []
    for d in dests:
        rid, pid = topo.addr(d)[:2]
        out.append(DstId(rid=rid, pnc=pid))
    return out


def helper_program(g, core, T, topo, r, dests):
    S = T.sem
    slot = slice(128 * r, 128 * r + 128)
    mask = common(topo, core, dests)
    n_in = engines(spare_engines(topo, T.cores[r], core, T.cores))
    ids = idents(topo, dests)
    for sem, ap in ((S.hs, T.ts[:, slot]), (S.hc, T.tq[:, slot].bitcast(dt.uint8))):
        g.wait_ge(sem, n_in)
        g.remote_dma_fused([RemoteDMATransfer(dst_ids=ids, dma_engine_mask=mask, remote_sem=S["arr%d" % r],
                                              src=ap, dsts=[ap for _ in ids])], local_sem=S.sent)
    g.wait_ge(S.sent, 2 * engines(mask))


def spare_engines(topo, src, near, cores):
    spare = topo.mask(src, near) & ~common(topo, src, [c for c in cores if c != src])
    bits = [b for b in range(spare.bit_length()) if spare >> b & 1]
    return sum(1 << b for b in bits[::2])


def rank_program(g, core, T, topo):
    cores = list(T.cores)
    rounds = plan(topo, cores)
    r = T.rank_of(core)
    if r is None:
        for j in range(N):
            if helper_of(topo, cores, j) == core:
                helper_program(g, core, T, topo, j, [cores[p[j]] for p in rounds[DIRECT:]])
        return
    S = T.sem
    A = ActivationFunctionType
    col = lambda k, w=128: slice(w * k, w * k + w)
    bank = lambda k: T.p[:, 512 * k:512 * k + 128]
    order = [r] + [p.index(r) for p in rounds]
    ybank = {j: k + 1 for k, j in enumerate(order)}
    ZB = 0

    g.sync.dma_start(T.xe[:, 0:512], T.x[:, :]).then_inc(S.ldx, 16)
    g.scalar.dma_start(T.xe[:, 512:1024], T.e[:, :]).then_inc(S.lde, 16)
    for i in range(4):
        q = g.sync if i % 2 == 0 else g.scalar
        q.dma_start(T.ab[:, col(i, 512)], T.a[:, col(i, 512)]).then_inc(S["lda%d" % i], 16)
    g.sync.dma_start(T.wb[:, :], T.w[:, :]).then_inc(S.ldw, 16)
    g.scalar.dma_start(T.vb[:, :], T.v[:, :]).then_inc(S.ldv, 16)

    v = g.vector

    def pack(i):
        v.wait_ge(S["lda%d" % i], 16)
        v.quantize_mx(T.aq[:, col(i)], T.asc[:, col(i)], T.ab[:, col(i, 512)]).then_inc(S["qa%d" % i], 1)

    def factor(i):
        v.wait_ge(S["um%d" % i], 1)
        v.tensor_scalar(T.m[:, col(i)], bank(i), 0.0, C, AluOpType.is_gt, AluOpType.mult).then_inc(S["m%d" % i], 1)

    def times(i):
        v.wait_ge(S["m%d" % i], 1)
        v.wait_ge(S["mm%d" % i], 1)
        v.tensor_tensor(T.t[:, i:512:4], bank(4 + i), T.m[:, col(i)], AluOpType.mult).then_inc(S["op%d" % i], 1)

    v.wait_ge(S.ldx, 16)
    v.quantize_mx(T.xq[:, 0:128], T.xs[:, 0:128], T.xe[:, 0:512]).then_inc(S.qx, 1)
    v.wait_ge(S.lde, 16)
    v.quantize_mx(T.xq[:, 128:256], T.xs[:, 128:256], T.xe[:, 512:1024]).then_inc(S.qe, 1)
    pack(0)
    pack(1)
    factor(0)
    pack(2)
    times(0)
    pack(3)
    times(1)
    factor(3)
    times(2)
    times(3)
    for i in range(4):
        v.wait_ge(S["op%d" % i], 1)
    v.quantize_mx(T.tq[:, col(r)], T.ts[:, col(r)], T.t[:, :]).then_inc(S.qt, 1)
    v.wait_ge(S.ldw, 16)
    v.quantize_mx(T.wq[:, :], T.ws[:, :], T.wb[:, :]).then_inc(S.qw, 1)
    v.wait_ge(S.ldv, 16)
    v.quantize_mx(T.vq[:, :], T.vs[:, :], T.vb[:, :]).then_inc(S.qv, 1)

    for n, i in enumerate(ON_SCALAR):
        g.scalar.wait_ge(S["um%d" % i], 1)
        g.scalar.activation(T.sg[:, col(n)], bank(i), A.Sign).then_inc(S["sg%d" % i], 1)
        g.scalar.wait_ge(S["sg%d" % i], 1)
        g.scalar.activation(T.m[:, col(i)], T.sg[:, col(n)], A.Relu, scale=C).then_inc(S["m%d" % i], 1)

    te = g.tensor
    te.wait_ge(S.qx, 1)
    for i in range(4):
        te.wait_ge(S["qa%d" % i], 1)
        w, ws = T.aq[:, col(i)], T.asc[:, col(i)]
        te.matmul_mx(bank(i), w, ws, T.xq[:, 0:128], T.xs[:, 0:128], True, True).then_inc(S["um%d" % i], 1)
        if i == 0:
            te.wait_ge(S.qe, 1)
        te.matmul_mx(bank(4 + i), w, ws, T.xq[:, 128:256], T.xs[:, 128:256], True, True).then_inc(S["mm%d" % i], 1)

    dests = [cores[p[r]] for p in rounds[:DIRECT]]
    near = helper_of(topo, cores, r)
    far_mask = common(topo, core, [c for c in cores if c != core])
    near_mask = spare_engines(topo, core, near, cores)
    ids, near_id = idents(topo, dests), idents(topo, [near])
    eng = engines(far_mask)
    g.wait_ge(S.qt, 1)
    for ap, sem in ((T.ts[:, col(r)], S.hs), (T.tq[:, col(r)].bitcast(dt.uint8), S.hc)):
        g.remote_dma_fused([RemoteDMATransfer(dst_ids=near_id, dma_engine_mask=near_mask, remote_sem=sem,
                                              src=ap, dsts=[ap]),
                            RemoteDMATransfer(dst_ids=ids, dma_engine_mask=far_mask, remote_sem=S["arr%d" % r],
                                              src=ap, dsts=[ap for _ in ids])], local_sem=S.sent)
    g.wait_ge(S.sent, 2 * (eng + engines(near_mask)))

    for k, j in enumerate(order):
        if k == 0:
            te.wait_ge(S.qt, 1)
            te.wait_ge(S.qw, 1)
        else:
            te.wait_ge(S["arr%d" % j], 2 * eng)
        q, s = T.tq[:, col(j)], T.ts[:, col(j)]
        te.matmul_mx(bank(ybank[j]), T.wq[:, :], T.ws[:, :], q, s, True, True).then_inc(S["ymm%d" % j], 1)
        if k == 0:
            te.wait_ge(S.qv, 1)
        mz = te.matmul_mx(bank(ZB), q, s, T.vq[:, :], T.vs[:, :], k == 0, k == N - 1)
        if k == N - 1:
            mz.then_inc(S.zmm, 1)

    nS = nA = 0
    for k, j in enumerate(order):
        y = T.yb[:, col(j)]
        if k % 2:
            v.wait_ge(S["ymm%d" % j], 1)
            v.tensor_copy(y, bank(ybank[j])).then_inc(S["yc%d" % j], 1)
            g.sync.wait_ge(S["yc%d" % j], 1)
            g.sync.dma_start(T.y[:, col(j)], y).then_inc(S.styS, 16)
            nS += 16
        else:
            g.scalar.wait_ge(S["ymm%d" % j], 1)
            g.scalar.activation(y, bank(ybank[j]), A.Copy).then_inc(S["yc%d" % j], 1)
            g.scalar.wait_ge(S["yc%d" % j], 1)
            g.scalar.dma_start(T.y[:, col(j)], y).then_inc(S.styA, 16)
            nA += 16
    v.wait_ge(S.zmm, 1)
    v.tensor_copy(T.zb[:, :], bank(ZB)).then_inc(S.zc, 1)
    g.sync.wait_ge(S.zc, 1)
    g.sync.dma_start(T.z[:, :], T.zb[:, :]).then_inc(S.styS, 16)
    nS += 16
    g.sync.wait_ge(S.styS, nS)
    g.scalar.wait_ge(S.styA, nA)
